import numpy as np, ml_dtypes
CORES = [0,1,2,3]
N = 4
GROUPS = [[0,1],[2,3]]
def setup_inputs(rng):
    return {"x": rng.standard_normal((N, 128, 2048), dtype=np.float32).astype(ml_dtypes.bfloat16)}
def reference(x):
    y = np.empty((N, 128, 1024), x.dtype)
    for g in GROUPS:
        s = x[g].sum(axis=0, dtype=np.float64).astype(x[g].dtype)
        n = len(g); b = x.shape[2] // n
        for i, r in enumerate(g):
            y[r] = s[:, i * b:(i + 1) * b]
    return {"y": y}

from concourse.mybir import AluOpType

ROWS = 128
WIDTH = 2048
SCRATCH = {
    "send": ("sbuf", [ROWS, WIDTH], "bfloat16"),
    "land": ("sbuf", [ROWS, WIDTH], "bfloat16"),
}
SEMAPHORES = ["local", "read", "arrived"]


def slot_of(owner, other):
    return other if other < owner else other - 1


def rank_program(g, core, T, topo):
    rank = T.rank_of(core)
    if rank is None:
        return
    group = [grp for grp in T.tables["GROUPS"] if rank in grp][0]
    n = len(group)
    i = group.index(rank)
    b = T.x.shape[1] // n
    others = [j for j in range(n) if j != i]

    done = 0
    for j in others:
        s = slot_of(i, j)
        g.dma_start(T.send[:, s * b:(s + 1) * b], T.x[:, j * b:(j + 1) * b]).then_inc(T.sem.local, 16)
        done += 16
    g.dma_start(T.y[:, :], T.x[:, i * b:(i + 1) * b]).then_inc(T.sem.local, 16)
    done += 16
    g.wait_ge(T.sem.local, done)

    for j in others:
        dst = T.cores[group[j]]
        rid, pid, sengine = topo.addr(dst)
        s, d = slot_of(i, j), slot_of(j, i)
        g.remote_dma(T.land[:, d * b:(d + 1) * b], T.send[:, s * b:(s + 1) * b],
                     T.sem.arrived, T.sem.read, pid, rid, topo.mask(core, dst))

    g.wait_ge(T.sem.arrived, 16 * (n - 1))
    for s in range(n - 1):
        g.dma_start(T.y[:, :], T.land[:, s * b:(s + 1) * b], accum_op=AluOpType.add).then_inc(T.sem.local, 16)
        done += 16
        g.wait_ge(T.sem.local, done)
    g.wait_ge(T.sem.read, 16 * (n - 1))
